import numpy as np
import ml_dtypes


def mxq(x, axis, fmt="e4m3"):
    dtype, down = {"e4m3": (ml_dtypes.float8_e4m3fn, 7), "e5m2": (ml_dtypes.float8_e5m2, 14)}[fmt]
    v = np.moveaxis(np.asarray(x, np.float32).astype(ml_dtypes.bfloat16).astype(np.float64), axis, -1)
    blocks = v.reshape(v.shape[:-1] + (-1, 32))
    amax = np.abs(blocks).max(-1, keepdims=True)
    byte = np.maximum(np.where(amax > 0, np.frexp(amax)[1] - 1 + 127, 0) - down, 1)
    scale = np.exp2(byte - 127.0)
    codes = (blocks / scale).astype(np.float32).astype(dtype).astype(np.float64)
    return np.moveaxis((codes * scale).reshape(v.shape), -1, axis)


WIDE = False


def mx_kscale(k):
    if not WIDE:
        return np.ones(k)
    levels = np.array([10, -10, 5, -5, 0])
    if k % 512:
        return np.exp2(np.random.permutation(np.resize(levels, k // 32))).repeat(32)
    a = np.empty((k // 512, 16))
    for p in range(k // 512):
        a[p, :8] = np.random.permutation(np.resize(levels, 8))
        for g in range(8):
            far = levels[np.abs(levels - a[p, g]) >= 10]
            a[p, g + 8] = far[np.random.randint(len(far))]
    return np.exp2(a.ravel()).repeat(32)


BF16 = ml_dtypes.bfloat16


def bf(x):
    return np.asarray(x, np.float32).astype(BF16)


def f64(x):
    return np.asarray(x).astype(np.float64)


E2M1 = np.array([0.0, 0.5, 1.0, 1.5, 2.0, 3.0, 4.0, 6.0, -0.0, -0.5, -1.0, -1.5, -2.0, -3.0, -4.0, -6.0])


def pack_weight(w, fmt):
    k, n = w.shape
    w = f64(bf(w)).reshape(k // 32, 32, n)
    amax = np.abs(w).max(1)
    if fmt == "e4m3":
        byte = np.frexp(amax)[1] - 1 + 127 - 7
    else:
        mant, ex = np.frexp(amax / 6.0)
        byte = np.where(mant > 0.5, ex, ex - 1) + 127
    byte = np.clip(np.where(amax > 0, byte, 1), 1, 254)
    scaled = (w * np.exp2(127.0 - byte)[:, None, :]).reshape(k, n).astype(np.float32)
    by_word = np.ascontiguousarray(scaled.reshape(k // 512, 128, 4, n).transpose(0, 1, 3, 2))
    if fmt == "e4m3":
        words = by_word.astype(ml_dtypes.float8_e4m3fn).view(np.uint8)
    else:
        c = by_word.astype(ml_dtypes.float4_e2m1fn).view(np.uint8) & 0xF
        words = c[..., 0::2] | (c[..., 1::2] << 4)
    return np.ascontiguousarray(words), np.ascontiguousarray(byte.astype(np.uint8).reshape(k // 512, 16, n))


def unpack_weight(words, scales, fmt):
    g, p, n, _ = words.shape
    if fmt == "e4m3":
        vals = np.ascontiguousarray(words).view(ml_dtypes.float8_e4m3fn).astype(np.float64)
    else:
        nib = np.empty((g, p, n, 4), np.uint8)
        nib[..., 0::2] = words & 0xF
        nib[..., 1::2] = words >> 4
        vals = E2M1[nib]
    vals = vals * np.repeat(np.exp2(scales.astype(np.float64) - 127.0), 8, axis=1)[..., None]
    return vals.transpose(0, 1, 3, 2).reshape(g * 512, n)

def planes(Y):
    n, m = Y.shape
    b = f64(bf(Y)).reshape(n // 32, 32, m)
    amax = np.abs(b).max(1)
    byte = np.clip(np.where(amax > 0, np.frexp(amax)[1] - 1 + 127 - 7, 1), 1, 254)
    codes = (b * np.exp2(127.0 - byte)[:, None, :]).reshape(n, m).astype(np.float32).astype(ml_dtypes.float8_e4m3fn).view(np.uint8)
    words = codes.reshape(n // 512, 128, 4, m).transpose(0, 1, 3, 2)
    return np.ascontiguousarray(words), np.ascontiguousarray(byte.astype(np.uint8).reshape(n // 512, 16, m))


T, D, F, V = 1024, 1024, 1024, 2048


def sigmoid(a):
    return 1.0 / (1.0 + np.exp(-a))


def setup_inputs():
    s = mx_kscale(D)
    u = mx_kscale(D)
    h = bf(np.random.standard_normal((T, D)) * s)
    t = bf(np.random.standard_normal((T, D)) * s)
    wa_words, wa_scales = pack_weight(np.random.standard_normal((D, F)) / np.sqrt(D) / s[:, None], "e4m3")
    wb_words, wb_scales = pack_weight(np.random.standard_normal((D, F)) / np.sqrt(D) / s[:, None], "e4m3")
    v = bf(np.random.standard_normal(F) * 1.5 / np.sqrt(F))
    gain = bf((1.0 + 0.1 * np.random.standard_normal(D)) * u / s)
    e_words, e_scales = pack_weight((np.random.standard_normal((V, D)) / np.sqrt(D) / u[None, :]).T, "e4m3")
    return {"h": h,
            "t": t,
            "wa_words": wa_words,
            "wa_scales": wa_scales,
            "wb_words": wb_words,
            "wb_scales": wb_scales,
            "v": v,
            "gain": gain,
            "e_words": e_words,
            "e_scales": e_scales}


def mixing_weight(h, t, wa, wb, v):
    a = mxq(h, 1, "e4m3") @ wa
    b = mxq(t, 1, "e4m3") @ wb
    r = np.maximum(a + b, 0.0)
    return sigmoid(np.sum(r * v, axis=-1))


def core(h, t, wa_words, wa_scales, wb_words, wb_scales, v, gain, e_words, e_scales):
    h, t, gain = f64(h), f64(t), f64(gain)
    wa = unpack_weight(wa_words, wa_scales, "e4m3")
    wb = unpack_weight(wb_words, wb_scales, "e4m3")
    w = mixing_weight(h, t, wa, wb, f64(v))
    m = h + w[:, None] * (t - h)
    mg = m * gain
    return mxq(mg, 1, "e4m3") @ unpack_weight(e_words, e_scales, "e4m3")


def reference(h, t, wa_words, wa_scales, wb_words, wb_scales, v, gain, e_words, e_scales):
    R_out = core(h, t, wa_words, wa_scales, wb_words, wb_scales, v, gain, e_words, e_scales)
    words, scales = planes(R_out)
    return R_out, words, scales

@@ -1,0 +1,392 @@
+from contextlib import ExitStack
+
+import concourse.mybir as mybir
+from concourse.masks import make_identity
+
+FLOPS = 2 * 1024 * 2048 * 1024 + 2 * 1024 * 1024 * 2048
+
+F32 = mybir.dt.float32
+BF16 = mybir.dt.bfloat16
+U32 = mybir.dt.uint32
+I32 = mybir.dt.int32
+U8 = mybir.dt.uint8
+FP8X4 = mybir.dt.float8_e4m3fn_x4
+ALU = mybir.AluOpType
+ACT = mybir.ActivationFunctionType
+
+P = 128
+D = 1024
+F = 1024
+V = 2048
+N = 512
+BLOCKS = 8
+BANKS = (3, 2, 3)
+PLAN = [('s2', 3, 1), ('quant', 3, 't'), ('s2', 2, 1), ('turn', 4, 'h'), ('s2', 4, 1), ('turn', 4, 't'), ('logits', 2, 0), ('gains', -1, 0), ('s2', 8, 1), ('fq', 5, 0), ('fq', 5, 0), ('logits', 2, 1), ('mix', 1, 0), ('fq', 7, 0), ('turn_mixed', -2, 0), ('gate', 2, 0), ('fq', 6, 0), ('fi', 9, 0), ('quant', -3, 'm'), ('fi', 5, 0), ('fi', 8, 0), ('quant', 4, 'h'), ('stage1', 3, 0), ('stage1', 3, 1)]
+F_ON_S = (6, 7)
+STEPS = range(-4, 20)
+EARLY = ()
+PERM = ()
+S2ORD = ("b", "b")
+
+
+def tile_quietstarthoughtmixinghead_x2_kernel(
+    tc, h, t, wa_words, wa_scales, wb_words, wb_scales, v, gain, e_words, e_scales, out_0, out_1, out_2
+):
+    nc = tc.nc
+    with ExitStack() as ctx:
+        keep = ctx.enter_context(tc.tile_pool(name="keep", bufs=1))
+        work = ctx.enter_context(tc.tile_pool(name="work", bufs=3))
+        psum = ctx.enter_context(tc.psum_pool(name="psum", bufs=1))
+        ctx.enter_context(tc.manual_schedule())
+
+        w_sc = keep.tile([P, F], U8, align_bytes=64, name="w_sc")
+        e_sc = keep.tile([P, V], U8, align_bytes=64, name="e_sc")
+        vg_row = keep.tile([P, 2 * D], BF16, align_bytes=64, name="vg_row")
+        ones = keep.tile([P, P], BF16, align_bytes=64, name="ones")
+        warm = keep.tile([P, 1], F32, align_bytes=64, name="warm")
+        warm_out = keep.tile([P, 1], F32, align_bytes=64, name="warm_out")
+        ident = keep.tile([P, P], F32, align_bytes=64, name="ident")
+        v_b = keep.tile([P, F], BF16, align_bytes=64, name="v_b")
+        gain_b = keep.tile([P, D], BF16, align_bytes=64, name="gain_b")
+
+        nc.vector.memset(w_sc[:].bitcast(I32), 0)
+        nc.vector.memset(vg_row[:], 0.0)
+        nc.vector.memset(warm[:], 0.0)
+        nc.vector.memset(e_sc[:].bitcast(I32), 0)
+        nc.vector.memset(ones[:], 1.0)
+
+        def load_rows(src, g, pair, nm):
+            dst = keep.tile([P, 2, D], BF16, align_bytes=64, name=nm)
+            view = src[512 * g : 512 * g + 512, :].rearrange("(p s) c -> p s c", s=4)
+            nc.sync.dma_start(out=dst[:], in_=view[:, 2 * pair : 2 * pair + 2, :])
+            return dst
+
+        def load_words(src, n, nm):
+            dst = keep.tile([P, 2, N], U32, align_bytes=64, name=nm)
+            view = src.rearrange("g p n b -> p g (n b)")[:, :, 4 * N * n : 4 * N * (n + 1)]
+            nc.sync.dma_start(out=dst[:].bitcast(I32), in_=view.bitcast(I32))
+            return dst
+
+        h_sb, t_sb, wa_sb, wb_sb, e_sb = {}, {}, {}, {}, {}
+        make_identity(nc, ident[:])
+        nc.scalar.dma_start(out=vg_row[0:1, 0:F], in_=v.unsqueeze(0))
+        for q in range(4):
+            nc.scalar.dma_start(
+                out=w_sc[32 * q : 32 * q + 8, :].bitcast(I32), in_=wa_scales[:, 4 * q : 4 * q + 4, :].bitcast(I32)
+            )
+        for q in range(4):
+            nc.gpsimd.dma_start(
+                out=w_sc[32 * q + 8 : 32 * q + 16, :].bitcast(I32),
+                in_=wb_scales[:, 4 * q : 4 * q + 4, :].bitcast(I32),
+            )
+        nc.gpsimd.dma_start(out=vg_row[0:1, F : F + D], in_=gain.unsqueeze(0))
+        for q in range(4):
+            nc.gpsimd.dma_start(
+                out=e_sc[32 * q : 32 * q + 8, :].bitcast(I32), in_=e_scales[:, 4 * q : 4 * q + 4, :].bitcast(I32)
+            )
+        h_sb[0] = load_rows(h, 0, 0, "h_sb0")
+        t_sb[0] = load_rows(t, 0, 0, "t_sb0")
+        wa_sb[0] = load_words(wa_words, 0, "wa_sb0")
+        wb_sb[0] = load_words(wb_words, 0, "wb_sb0")
+        wa_sb[1] = load_words(wa_words, 1, "wa_sb1")
+        wb_sb[1] = load_words(wb_words, 1, "wb_sb1")
+        h_sb[1] = load_rows(h, 0, 1, "h_sb1")
+        t_sb[1] = load_rows(t, 0, 1, "t_sb1")
+        h_sb[2] = load_rows(h, 1, 0, "h_sb2")
+        t_sb[2] = load_rows(t, 1, 0, "t_sb2")
+        for n in range(4):
+            e_sb[n] = load_words(e_words, n, "e_sb%d" % n)
+        h_sb[3] = load_rows(h, 1, 1, "h_sb3")
+        t_sb[3] = load_rows(t, 1, 1, "t_sb3")
+        rows = {"h": h_sb, "t": t_sb}
+        weights = {"h": wa_sb, "t": wb_sb}
+
+        nc.scalar.activation(out=warm_out[:], in_=warm[:], func=ACT.Sigmoid)
+
+        def row_of(x, b):
+            return rows[x][b // 2][:, b % 2, :]
+
+        grouped, codes, scales = {}, {}, {}
+
+        def copy_grouped(dst, bank):
+            nc.scalar.copy(
+                out=dst[:].bitcast(F32).rearrange("p (g r u) -> p g r u", g=2, u=2),
+                in_=bank[:].rearrange("p (g u r) -> p g r u", g=2, u=2),
+            )
+
+        permuted = {}
+
+        def perm(x, pair):
+            dst = work.tile([P, 2, 512], F32, align_bytes=64, name="pw", tag="pw", bufs=4)
+            nc.vector.tensor_copy(
+                out=dst[:].rearrange("p s (u k) -> p s u k", u=2),
+                in_=rows[x][pair][:].bitcast(F32).rearrange("p s (k u) -> p s u k", u=2),
+            )
+            permuted[x, pair] = dst
+
+        def turn(x, b):
+            if (x, b // 2) in permuted:
+                words = permuted[x, b // 2][:, b % 2, :]
+            else:
+                words = row_of(x, b).bitcast(F32)
+            bank = psum.tile([P, N], F32, name="bank_t", tag="bank_t", bufs=BANKS[0])
+            for g in range(2):
+                for u in range(2):
+                    lo = (2 * g + u) * P
+                    if (x, b // 2) in permuted:
+                        part = words[:, 256 * u + P * g : 256 * u + P * (g + 1)]
+                    else:
+                        part = words[:, 256 * g + u : 256 * (g + 1) : 2]
+                    nc.tensor.transpose(bank[:, lo : lo + P], part, ident[:])
+            dst = work.tile([P, D], BF16, align_bytes=64, name="gr", tag="gr", bufs=4)
+            copy_grouped(dst, bank)
+            grouped[x, b] = dst
+
+        def quant(x, b):
+            c = work.tile([P, 256], U32, align_bytes=64, name="cd", tag="cd", bufs=8)
+            s = work.tile([P, 256], U8, align_bytes=64, name="sc", tag="sc", bufs=8)
+            nc.vector.quantize_mx(out=c[:].bitcast(FP8X4), scales=s[:], in_=grouped[x, b][:])
+            codes[x, b], scales[x, b] = c, s
+
+        hidden, logit, w_t, a_t, m_t, mg_t = {}, {}, {}, {}, {}, {}
+
+        def stage1(b, hf):
+            acc = psum.tile([P, N], F32, name="bank_1", tag="bank_1", bufs=BANKS[1])
+            cols = slice(N * hf, N * (hf + 1))
+            for i, x in enumerate("ht"):
+                for g in range(2):
+                    k = 4 * (2 * i + g)
+                    nc.tensor.matmul_mx(
+                        out=acc[:],
+                        lhsT=codes[x, b][:, P * g : P * (g + 1)].bitcast(FP8X4),
+                        lhsT_scale=scales[x, b][:, P * g : P * (g + 1)],
+                        rhs=weights[x][hf][:, g, :].bitcast(FP8X4),
+                        rhs_scale=w_sc[k:P, cols],
+                        start=(k == 0),
+                        stop=(k == 12),
+                    )
+            hidden[b, hf] = acc
+
+        def logits(b, hf):
+            if hf == 0:
+                logit[b] = work.tile([P, 2], F32, align_bytes=64, name="lg", tag="lg", bufs=3)
+            junk = work.tile([P, N], F32, align_bytes=64, name="junk", tag="junk", bufs=2)
+            nc.vector.scalar_tensor_tensor(
+                out=junk[:],
+                in0=hidden[b, hf][:],
+                scalar=0.0,
+                in1=v_b[:, N * hf : N * (hf + 1)],
+                op0=ALU.max,
+                op1=ALU.mult,
+                accum_out=logit[b][:, hf : hf + 1],
+            )
+
+        def gate(b):
+            w = work.tile([P, 1], F32, align_bytes=64, name="wt", tag="wt", bufs=4)
+            u = work.tile([P, 1], F32, align_bytes=64, name="ut", tag="ut", bufs=3)
+            nc.scalar.activation(out=w[:], in_=logit[b][:, 0:1], func=ACT.Sigmoid, bias=logit[b][:, 1:2], scale=1.0)
+            nc.scalar.activation(out=u[:], in_=w[:], func=ACT.Copy, bias=1.0, scale=-1.0)
+            a = work.tile([P, D], F32, align_bytes=64, name="at", tag="at", bufs=3)
+            src = gained["h", b][:] if b in EARLY else row_of("h", b)
+            nc.scalar.activation(out=a[:], in_=src, func=ACT.Copy, scale=u[:, 0:1])
+            w_t[b], a_t[b] = w, a
+
+        gained = {}
+
+        def early_gain(x, b):
+            if b not in EARLY:
+                return
+            dst = work.tile([P, D], F32, align_bytes=64, name="eg", tag="eg", bufs=4)
+            nc.vector.tensor_tensor(
+                out=dst[:].rearrange("p (u k e) -> p u k e", u=2, e=2),
+                in0=row_of(x, b).rearrange("p (k u e) -> p u k e", u=2, e=2),
+                in1=gain_b[:].rearrange("p (u k e) -> p u k e", u=2, e=2),
+                op=ALU.mult,
+            )
+            gained[x, b] = dst
+
+        def mix(b):
+            if b in EARLY:
+                return
+            m = work.tile([P, D], F32, align_bytes=64, name="mt", tag="mt", bufs=3)
+            nc.vector.scalar_tensor_tensor(
+                out=m[:], in0=row_of("t", b), scalar=w_t[b][:, 0:1], in1=a_t[b][:], op0=ALU.mult, op1=ALU.add
+            )
+            m_t[b] = m
+
+        def gains(b):
+            mg = work.tile([P, D], BF16, align_bytes=64, name="mg", tag="mg", bufs=3)
+            mg_t[b] = mg
+            if b in EARLY:
+                nc.vector.scalar_tensor_tensor(
+                    out=mg[:], in0=gained["t", b][:], scalar=w_t[b][:, 0:1], in1=a_t[b][:], op0=ALU.mult, op1=ALU.add
+                )
+                return
+            nc.vector.tensor_tensor(
+                out=mg[:].rearrange("p (u k e) -> p u k e", u=2, e=2),
+                in0=m_t[b][:].rearrange("p (k u e) -> p u k e", u=2, e=2),
+                in1=gain_b[:].rearrange("p (u k e) -> p u k e", u=2, e=2),
+                op=ALU.mult,
+            )
+
+        def turn_mixed(b):
+            words = mg_t[b][:].bitcast(F32)
+            bank = psum.tile([P, N], F32, name="bank_t", tag="bank_t", bufs=BANKS[0])
+            for g in range(2):
+                for u in range(2):
+                    lo = (2 * g + u) * P
+                    nc.tensor.transpose(bank[:, lo : lo + P], words[:, 256 * u + P * g : 256 * u + P * (g + 1)], ident[:])
+            dst = work.tile([P, D], BF16, align_bytes=64, name="gm", tag="gm", bufs=3)
+            copy_grouped(dst, bank)
+            grouped["m", b] = dst
+
+        out_f, out_s = {}, {}
+        stored = set()
+
+        def stage2(b, n):
+            g, s = divmod(b, 4)
+            if g not in out_f:
+                out_f[g] = keep.tile([P, 4, V], F32, align_bytes=64, name="out_f%d" % g)
+                out_s[g] = keep.tile([P, V], U8, align_bytes=64, name="out_s%d" % g)
+            acc = psum.tile([P, N], F32, name="bank_2", tag="bank_2", bufs=BANKS[2])
+            cols = slice(N * n, N * (n + 1))
+            for k in range(2):
+                nc.tensor.matmul_mx(
+                    out=acc[:],
+                    lhsT=codes["m", b][:, P * k : P * (k + 1)].bitcast(FP8X4),
+                    lhsT_scale=scales["m", b][:, P * k : P * (k + 1)],
+                    rhs=e_sb[n][:, k, :].bitcast(FP8X4),
+                    rhs_scale=e_sc[4 * k : P, cols],
+                    start=(k == 0),
+                    stop=(k == 1),
+                )
+            nc.scalar.copy(out=out_f[g][:, s, cols], in_=acc[:])
+            stored.add((b, n))
+            view = out_0[512 * g : 512 * g + 512, :].rearrange("(p s) m -> p s m", s=4)
+            if S2ORD[g] == "chunk":
+                if s == 3:
+                    nc.sync.dma_start(out=view[:, :, cols], in_=out_f[g][:, :, cols])
+            elif n % 2 == 1:
+                pair = slice(N * (n - 1), N * (n + 1))
+                nc.sync.dma_start(out=view[:, s, pair], in_=out_f[g][:, s, pair])
+
+        out_b = {}
+
+        def interleave(g, n, engine):
+            ob = work.tile([P, N, 4], BF16, align_bytes=64, name="ob", tag="ob", bufs=3)
+            engine(
+                out=ob[:], in_=out_f[g][:, :, N * n : N * (n + 1)].rearrange("p s m -> p m s")
+            )
+            out_b[g, n] = ob
+
+        def quant_out(g, n):
+            oc = work.tile([P, N], U32, align_bytes=64, name="oc", tag="oc", bufs=6)
+            nc.vector.quantize_mx(
+                out=oc[:].bitcast(FP8X4),
+                scales=out_s[g][:, N * n : N * (n + 1)],
+                in_=out_b[g, n][:].rearrange("p m s -> p (m s)"),
+            )
+            view = out_1[g].rearrange("p m b -> p (m b)")[:, 4 * N * n : 4 * N * (n + 1)]
+            nc.sync.dma_start(out=view.bitcast(I32), in_=oc[:].bitcast(I32))
+            if n == 3:
+                for q in range(4):
+                    nc.sync.dma_start(
+                        out=out_2[g, 4 * q : 4 * q + 4, :].bitcast(I32),
+                        in_=out_s[g][32 * q : 32 * q + 4, :].bitcast(I32),
+                    )
+
+        def spread():
+            for c in (2, 3, 0, 1):
+                bank = psum.tile([P, N], F32, name="bank_t", tag="bank_t", bufs=BANKS[0])
+                nc.tensor.matmul(bank[:], lhsT=ones[:], rhs=vg_row[:, N * c : N * (c + 1)], start=True, stop=True)
+                if c < 2:
+                    nc.scalar.copy(out=v_b[:, N * c : N * (c + 1)], in_=bank[:])
+                else:
+                    nc.scalar.copy(
+                        out=gain_b[:].rearrange("p (u g k e) -> p u g k e", u=2, g=2, e=2)[:, :, c - 2, :, :],
+                        in_=bank[:].rearrange("p (k u e) -> p u k e", u=2, e=2),
+                    )
+
+        done = []
+        stream = []
+        for g in range(2):
+            if S2ORD[g] == "b":
+                stream += [(4 * g + s, n) for s in range(4) for n in range(4)]
+            elif S2ORD[g] == "late":
+                stream += [(4 * g + s, n) for s in range(2) for n in range(4)]
+                stream += [(4 * g + s, n) for n in range(4) for s in (2, 3)]
+            elif S2ORD[g] == "late3":
+                stream += [(4 * g + s, n) for s in range(1) for n in range(4)]
+                stream += [(4 * g + s, n) for n in range(4) for s in (1, 2, 3)]
+            elif S2ORD[g] == "pair":
+                stream += [(4 * g + s, 2 * c + n) for c in range(2) for s in range(4) for n in range(2)]
+            else:
+                stream += [(4 * g + s, n) for n in range(4) for s in range(4)]
+        late_i = []
+        late_q = []
+
+        def fill_i():
+            i = len(late_i)
+            if i < 8 and all((4 * (i // 4) + s, i % 4) in stored for s in range(4)):
+                g, n = divmod(i, 4)
+                interleave(g, n, nc.scalar.copy if i in F_ON_S else nc.vector.tensor_copy)
+                late_i.append(i)
+
+        def fill_q():
+            i = len(late_q)
+            if i < len(late_i):
+                quant_out(*divmod(i, 4))
+                late_q.append(i)
+
+        for k in STEPS:
+            for piece, off, arg in PLAN:
+                b = k + off
+                if piece == "fi":
+                    if k >= off:
+                        fill_i()
+                    continue
+                if piece == "fq":
+                    if k >= off:
+                        fill_q()
+                    continue
+                if piece == "s2":
+                    for i in range(arg):
+                        if k >= off and stream and ("m", stream[0][0]) in codes:
+                            stage2(*stream.pop(0))
+                    continue
+                if piece == "perm":
+                    if b % 2 == 0 and b // 2 in PERM and 0 <= b < BLOCKS:
+                        perm(arg, b // 2)
+                    continue
+                if not 0 <= b < BLOCKS:
+                    continue
+                if piece == "turn":
+                    turn(arg, b)
+                elif piece == "quant":
+                    quant(arg, b)
+                elif piece == "pre":
+                    if not done:
+                        spread()
+                        done.append(1)
+                    early_gain(arg, b)
+                elif piece == "stage1":
+                    if not done:
+                        spread()
+                        done.append(1)
+                    stage1(b, arg)
+                elif piece == "logits":
+                    logits(b, arg)
+                elif piece == "gate":
+                    gate(b)
+                elif piece == "mix":
+                    mix(b)
+                elif piece == "gains":
+                    gains(b)
+                elif piece == "turn_mixed":
+                    turn_mixed(b)
+        while len(late_q) < 8:
+            if stream:
+                stage2(*stream.pop(0))
+                continue
+            fill_i()
+            fill_q()

@@ -21,11 +21,12 @@ V = 2048
 N = 512
 BLOCKS = 8
 BANKS = (3, 2, 3)
-PLAN = [('s2', 3, 1), ('quant', 3, 't'), ('s2', 2, 1), ('turn', 4, 'h'), ('s2', 4, 1), ('turn', 4, 't'), ('logits', 2, 0), ('gains', -1, 0), ('s2', 8, 1), ('fq', 5, 0), ('fq', 5, 0), ('logits', 2, 1), ('mix', 1, 0), ('fq', 7, 0), ('turn_mixed', -2, 0), ('gate', 2, 0), ('fq', 6, 0), ('fi', 9, 0), ('quant', -3, 'm'), ('fi', 5, 0), ('fi', 8, 0), ('quant', 4, 'h'), ('stage1', 3, 0), ('stage1', 3, 1)]
-F_ON_S = (6, 7)
+PLAN = [('turn', 2, 't'), ('s2', 5, 1), ('logits', -1, 0), ('s2', -8, 1), ('quant', -5, 'm'), ('fi', 13, 0), ('quant', 2, 'h'), ('fq', 3, 0), ('logits', -1, 1), ('turn', 3, 'h'), ('mix', -2, 0), ('gate', -1, 0), ('pre', -14, 't'), ('fi', 0, 0), ('quant', 2, 't'), ('gains', -2, 0), ('turn_mixed', -3, 0), ('stage1', 0, 0), ('s2', -1, 1), ('pre', 2, 'h'), ('stage1', 0, 1)]
+F_ON_S = (7,)
 STEPS = range(-4, 20)
 EARLY = ()
 PERM = ()
+LOADS = "B"
 S2ORD = ("b", "b")
 
 
@@ -69,35 +70,49 @@ def tile_quietstarthoughtmixinghead_x2_kernel(
 
         h_sb, t_sb, wa_sb, wb_sb, e_sb = {}, {}, {}, {}, {}
         make_identity(nc, ident[:])
-        nc.scalar.dma_start(out=vg_row[0:1, 0:F], in_=v.unsqueeze(0))
         for q in range(4):
             nc.scalar.dma_start(
                 out=w_sc[32 * q : 32 * q + 8, :].bitcast(I32), in_=wa_scales[:, 4 * q : 4 * q + 4, :].bitcast(I32)
             )
-        for q in range(4):
-            nc.gpsimd.dma_start(
-                out=w_sc[32 * q + 8 : 32 * q + 16, :].bitcast(I32),
-                in_=wb_scales[:, 4 * q : 4 * q + 4, :].bitcast(I32),
-            )
-        nc.gpsimd.dma_start(out=vg_row[0:1, F : F + D], in_=gain.unsqueeze(0))
-        for q in range(4):
-            nc.gpsimd.dma_start(
-                out=e_sc[32 * q : 32 * q + 8, :].bitcast(I32), in_=e_scales[:, 4 * q : 4 * q + 4, :].bitcast(I32)
-            )
-        h_sb[0] = load_rows(h, 0, 0, "h_sb0")
-        t_sb[0] = load_rows(t, 0, 0, "t_sb0")
-        wa_sb[0] = load_words(wa_words, 0, "wa_sb0")
-        wb_sb[0] = load_words(wb_words, 0, "wb_sb0")
-        wa_sb[1] = load_words(wa_words, 1, "wa_sb1")
-        wb_sb[1] = load_words(wb_words, 1, "wb_sb1")
-        h_sb[1] = load_rows(h, 0, 1, "h_sb1")
-        t_sb[1] = load_rows(t, 0, 1, "t_sb1")
-        h_sb[2] = load_rows(h, 1, 0, "h_sb2")
-        t_sb[2] = load_rows(t, 1, 0, "t_sb2")
-        for n in range(4):
-            e_sb[n] = load_words(e_words, n, "e_sb%d" % n)
-        h_sb[3] = load_rows(h, 1, 1, "h_sb3")
-        t_sb[3] = load_rows(t, 1, 1, "t_sb3")
+        nc.scalar.dma_start(out=vg_row[0:1, 0:F], in_=v.unsqueeze(0))
+        nc.scalar.dma_start(out=vg_row[0:1, F : F + D], in_=gain.unsqueeze(0))
+
+        def load_pair(i):
+            h_sb[i] = load_rows(h, i // 2, i % 2, "h_sb%d" % i)
+            t_sb[i] = load_rows(t, i // 2, i % 2, "t_sb%d" % i)
+
+        def load_weights(n):
+            wa_sb[n] = load_words(wa_words, n, "wa_sb%d" % n)
+            wb_sb[n] = load_words(wb_words, n, "wb_sb%d" % n)
+
+        def load_wb_scales():
+            for q in range(4):
+                nc.sync.dma_start(
+                    out=w_sc[32 * q + 8 : 32 * q + 16, :].bitcast(I32),
+                    in_=wb_scales[:, 4 * q : 4 * q + 4, :].bitcast(I32),
+                )
+
+        def load_e():
+            for q in range(4):
+                nc.sync.dma_start(
+                    out=e_sc[32 * q : 32 * q + 8, :].bitcast(I32), in_=e_scales[:, 4 * q : 4 * q + 4, :].bitcast(I32)
+                )
+            for n in range(4):
+                e_sb[n] = load_words(e_words, n, "e_sb%d" % n)
+
+        load_pair(0)
+        load_wb_scales()
+        if LOADS == "B":
+            load_pair(1)
+            load_weights(0)
+            load_weights(1)
+        else:
+            load_weights(0)
+            load_weights(1)
+            load_pair(1)
+        load_pair(2)
+        load_e()
+        load_pair(3)
         rows = {"h": h_sb, "t": t_sb}
         weights = {"h": wa_sb, "t": wb_sb}
 
@@ -117,7 +132,7 @@ def tile_quietstarthoughtmixinghead_x2_kernel(
         permuted = {}
 
         def perm(x, pair):
-            dst = work.tile([P, 2, 512], F32, align_bytes=64, name="pw", tag="pw", bufs=4)
+            dst = work.tile([P, 2, 512], F32, align_bytes=64, name="pw", tag="pw", bufs=2)
             nc.vector.tensor_copy(
                 out=dst[:].rearrange("p s (u k) -> p s u k", u=2),
                 in_=rows[x][pair][:].bitcast(F32).rearrange("p s (k u) -> p s u k", u=2),
@@ -184,8 +199,8 @@ def tile_quietstarthoughtmixinghead_x2_kernel(
         def gate(b):
             w = work.tile([P, 1], F32, align_bytes=64, name="wt", tag="wt", bufs=4)
             u = work.tile([P, 1], F32, align_bytes=64, name="ut", tag="ut", bufs=3)
-            nc.scalar.activation(out=w[:], in_=logit[b][:, 0:1], func=ACT.Sigmoid, bias=logit[b][:, 1:2], scale=1.0)
-            nc.scalar.activation(out=u[:], in_=w[:], func=ACT.Copy, bias=1.0, scale=-1.0)
+            nc.scalar.activation(out=u[:], in_=logit[b][:, 0:1], func=ACT.Sigmoid, bias=logit[b][:, 1:2], scale=-1.0)
+            nc.scalar.activation(out=w[:], in_=logit[b][:, 1:2], func=ACT.Sigmoid, bias=logit[b][:, 0:1], scale=-1.0)
             a = work.tile([P, D], F32, align_bytes=64, name="at", tag="at", bufs=3)
             src = gained["h", b][:] if b in EARLY else row_of("h", b)
             nc.scalar.activation(out=a[:], in_=src, func=ACT.Copy, scale=u[:, 0:1])
@@ -280,7 +295,7 @@ def tile_quietstarthoughtmixinghead_x2_kernel(
             out_b[g, n] = ob
 
         def quant_out(g, n):
-            oc = work.tile([P, N], U32, align_bytes=64, name="oc", tag="oc", bufs=6)
+            oc = work.tile([P, N], U32, align_bytes=64, name="oc", tag="oc", bufs=4)
             nc.vector.quantize_mx(
                 out=oc[:].bitcast(FP8X4),
                 scales=out_s[g][:, N * n : N * (n + 1)],
@@ -296,11 +311,13 @@ def tile_quietstarthoughtmixinghead_x2_kernel(
                     )
 
         def spread():
-            for c in (2, 3, 0, 1):
+            for c in range(4):
                 bank = psum.tile([P, N], F32, name="bank_t", tag="bank_t", bufs=BANKS[0])
                 nc.tensor.matmul(bank[:], lhsT=ones[:], rhs=vg_row[:, N * c : N * (c + 1)], start=True, stop=True)
-                if c < 2:
-                    nc.scalar.copy(out=v_b[:, N * c : N * (c + 1)], in_=bank[:])
+                if c == 0:
+                    nc.scalar.copy(out=v_b[:, 0:N], in_=bank[:])
+                elif c == 1:
+                    nc.scalar.activation(out=v_b[:, N:F], in_=bank[:], func=ACT.Copy, scale=-1.0)
                 else:
                     nc.scalar.copy(
                         out=gain_b[:].rearrange("p (u g k e) -> p u g k e", u=2, g=2, e=2)[:, :, c - 2, :, :],

@@ -21,12 +21,13 @@ V = 2048
 N = 512
 BLOCKS = 8
 BANKS = (3, 2, 3)
-PLAN = [('turn', 2, 't'), ('s2', 5, 1), ('logits', -1, 0), ('s2', -8, 1), ('quant', -5, 'm'), ('fi', 13, 0), ('quant', 2, 'h'), ('fq', 3, 0), ('logits', -1, 1), ('turn', 3, 'h'), ('mix', -2, 0), ('gate', -1, 0), ('pre', -14, 't'), ('fi', 0, 0), ('quant', 2, 't'), ('gains', -2, 0), ('turn_mixed', -3, 0), ('stage1', 0, 0), ('s2', -1, 1), ('pre', 2, 'h'), ('stage1', 0, 1)]
+PLAN = [('gate', -6, 0), ('fq', 2, 0), ('mix', -7, 0), ('quant', -9, 'm'), ('logits', -5, 0), ('s2', 10, 1), ('turn_mixed', -8, 0), ('fi', 10, 0), ('s2', 8, 1), ('gains', -7, 0), ('fq', 5, 0), ('s2', 4, 1), ('s2', -1, 1), ('quant', -2, 'h'), ('stage1', -4, 0), ('turn', -1, 'h'), ('fq', 3, 0), ('fq', 11, 0), ('quant', -2, 't'), ('turn', -1, 't'), ('logits', -5, 1), ('stage1', -4, 1)]
 F_ON_S = (7,)
 STEPS = range(-4, 20)
 EARLY = ()
 PERM = ()
 LOADS = "B"
+WIDE = 6
 S2ORD = ("b", "b")
 
 
@@ -62,9 +63,9 @@ def tile_quietstarthoughtmixinghead_x2_kernel(
             nc.sync.dma_start(out=dst[:], in_=view[:, 2 * pair : 2 * pair + 2, :])
             return dst
 
-        def load_words(src, n, nm):
-            dst = keep.tile([P, 2, N], U32, align_bytes=64, name=nm)
-            view = src.rearrange("g p n b -> p g (n b)")[:, :, 4 * N * n : 4 * N * (n + 1)]
+        def load_words(src, n, nm, width=N):
+            dst = keep.tile([P, 2, width], U32, align_bytes=64, name=nm)
+            view = src.rearrange("g p n b -> p g (n b)")[:, :, 4 * width * n : 4 * width * (n + 1)]
             nc.sync.dma_start(out=dst[:].bitcast(I32), in_=view.bitcast(I32))
             return dst
 
@@ -97,12 +98,27 @@ def tile_quietstarthoughtmixinghead_x2_kernel(
                 nc.sync.dma_start(
                     out=e_sc[32 * q : 32 * q + 8, :].bitcast(I32), in_=e_scales[:, 4 * q : 4 * q + 4, :].bitcast(I32)
                 )
-            for n in range(4):
-                e_sb[n] = load_words(e_words, n, "e_sb%d" % n)
+            for n in range(2):
+                e_sb[n] = load_words(e_words, n, "e_sb%d" % n, 2 * N)
 
-        load_pair(0)
-        load_wb_scales()
-        if LOADS == "B":
+        if LOADS == "C":
+            for nm, src, group in (("h", h, h_sb), ("t", t, t_sb)):
+                group[0] = keep.tile([P, 2, D], BF16, align_bytes=64, name="%s_sb0" % nm)
+                view = src[0:512, :].rearrange("(p s) c -> p s c", s=4)
+                nc.sync.dma_start(out=group[0][:, 0, :], in_=view[:, 0, :])
+            load_wb_scales()
+            load_weights(0)
+            for src, group in ((h, h_sb), (t, t_sb)):
+                view = src[0:512, :].rearrange("(p s) c -> p s c", s=4)
+                nc.sync.dma_start(out=group[0][:, 1, :], in_=view[:, 1, :])
+            load_weights(1)
+            load_pair(1)
+        else:
+            load_pair(0)
+            load_wb_scales()
+        if LOADS == "C":
+            pass
+        elif LOADS == "B":
             load_pair(1)
             load_weights(0)
             load_weights(1)
@@ -270,7 +286,7 @@ def tile_quietstarthoughtmixinghead_x2_kernel(
                     out=acc[:],
                     lhsT=codes["m", b][:, P * k : P * (k + 1)].bitcast(FP8X4),
                     lhsT_scale=scales["m", b][:, P * k : P * (k + 1)],
-                    rhs=e_sb[n][:, k, :].bitcast(FP8X4),
+                    rhs=e_sb[n // 2][:, k, N * (n % 2) : N * (n % 2 + 1)].bitcast(FP8X4),
                     rhs_scale=e_sc[4 * k : P, cols],
                     start=(k == 0),
                     stop=(k == 1),
@@ -281,28 +297,39 @@ def tile_quietstarthoughtmixinghead_x2_kernel(
             if S2ORD[g] == "chunk":
                 if s == 3:
                     nc.sync.dma_start(out=view[:, :, cols], in_=out_f[g][:, :, cols])
-            elif n % 2 == 1:
+            elif b < WIDE and n == 3:
+                nc.sync.dma_start(out=view[:, s, :], in_=out_f[g][:, s, :])
+            elif b >= WIDE and n % 2 == 1:
                 pair = slice(N * (n - 1), N * (n + 1))
                 nc.sync.dma_start(out=view[:, s, pair], in_=out_f[g][:, s, pair])
 
-        out_b = {}
+        out_b, out_c = {}, {}
 
         def interleave(g, n, engine):
             ob = work.tile([P, N, 4], BF16, align_bytes=64, name="ob", tag="ob", bufs=3)
             engine(
-                out=ob[:], in_=out_f[g][:, :, N * n : N * (n + 1)].rearrange("p s m -> p m s")
+                out=ob[:].rearrange("p (c i) s -> p c s i", i=4),
+                in_=out_f[g][:, :, N * n : N * (n + 1)].rearrange("p s (c i) -> p c s i", i=4),
             )
             out_b[g, n] = ob
 
         def quant_out(g, n):
-            oc = work.tile([P, N], U32, align_bytes=64, name="oc", tag="oc", bufs=4)
+            if n % 2 == 0:
+                out_c[g] = work.tile([P, 2 * N], U32, align_bytes=64, name="oc", tag="oc", bufs=2)
+            half = slice(N * (n % 2), N * (n % 2 + 1))
+            oc = out_c[g]
             nc.vector.quantize_mx(
-                out=oc[:].bitcast(FP8X4),
+                out=oc[:, half].bitcast(FP8X4),
                 scales=out_s[g][:, N * n : N * (n + 1)],
                 in_=out_b[g, n][:].rearrange("p m s -> p (m s)"),
             )
-            view = out_1[g].rearrange("p m b -> p (m b)")[:, 4 * N * n : 4 * N * (n + 1)]
-            nc.sync.dma_start(out=view.bitcast(I32), in_=oc[:].bitcast(I32))
+            words_view = out_1[g].rearrange("p m b -> p (m b)")
+            if (g, n) in ((1, 2), (1, 3)):
+                part = words_view[:, 4 * N * n : 4 * N * (n + 1)]
+                nc.sync.dma_start(out=part.bitcast(I32), in_=oc[:, half].bitcast(I32))
+            elif n % 2 == 1:
+                part = words_view[:, 4 * N * (n - 1) : 4 * N * (n + 1)]
+                nc.sync.dma_start(out=part.bitcast(I32), in_=oc[:].bitcast(I32))
             if n == 3:
                 for q in range(4):
                     nc.sync.dma_start(

@@ -21,14 +21,27 @@ V = 2048
 N = 512
 BLOCKS = 8
 BANKS = (3, 2, 3)
-PLAN = [('gate', -6, 0), ('fq', 2, 0), ('mix', -7, 0), ('quant', -9, 'm'), ('logits', -5, 0), ('s2', 10, 1), ('turn_mixed', -8, 0), ('fi', 10, 0), ('s2', 8, 1), ('gains', -7, 0), ('fq', 5, 0), ('s2', 4, 1), ('s2', -1, 1), ('quant', -2, 'h'), ('stage1', -4, 0), ('turn', -1, 'h'), ('fq', 3, 0), ('fq', 11, 0), ('quant', -2, 't'), ('turn', -1, 't'), ('logits', -5, 1), ('stage1', -4, 1)]
-F_ON_S = (7,)
-STEPS = range(-4, 20)
+LOADS = "C"
+F_ON_S = (6,)
 EARLY = ()
-PERM = ()
-LOADS = "B"
-WIDE = 6
-S2ORD = ("b", "b")
+BUFS = dict(gr=5, hq=10, at=3, mt=2, mg=3, gm=3, mq=6, ob=4, eg=4)
+ORDER = """
+    Th0 Tt0 Gh0 Gt0 sp1 sp0 Qt0 Qh0 U00 W00 sp2 spc1 spc0 spc2 Th1 Tt1
+    U01 sp3 W01 Gh1 Gt1 spc3 L00 Qh1 L01 Qt1 U11 Th3 U10 W10 Th2 Tt2
+    g0 A0 Gh3 Gh2 Gt2 Tt3 W11 m0 Qh3 Qh2 L10 L11 Gt3 Th5 Th4 Tt4
+    U21 Gt4 Gh5 Gh4 g1 A1 Qt2 n0 Qt4 Qt3 U20 W21 W20 Tt5 M0 L21
+    L20 m1 U31 W31 U30 g2 Gm0 Gt5 Th7 Th6 Tt6 Gh7 Gh6 A2 Qm0 L31
+    Qh5 Qh4 n1 W30 S02 S00 U41 S03 Qt5 Qh7 L30 m2 n2 W41 U40 W40
+    O00 g3 O02 Gt6 O03 A3 Tt7 M1 M2 L41 Qt6 L40 m3 U51 W51 U50
+    W50 S01 Gm1 g4 Gm2 Gt7 A4 Qm1 Qh6 L51 L50 n3 m4 Qm2 S12 S13
+    U61 U60 W61 W60 L61 L60 Qt7 n4 O12 O01 O13 g5 A5 M3 S23 S22
+    S11 U70 g6 O23 O22 A6 Gm3 O11 m5 n5 S10 S21 W70 U71 W71 S20
+    O21 O10 O20 M4 M5 L70 Qm3 L71 Gm4 Gm5 g7 m6 Qm4 n6 Qm5 S33
+    S43 S32 O33 A7 O43 O32 S53 M6 F3 m7 S31 O53 Gm6 S42 S52 O31
+    O42 S41 F2 Qm6 O52 S30 O41 S63 O30 S62 O63 n7 X2 O62 S40 M7
+    S51 S61 O40 Gm7 O51 S60 S50 O61 O60 O50 X3 F1 Qm7 F0 X1 X0
+    S73 S70 S71 O73 O70 S72 F7 O71 O72 F4 F5 F6 X7 X6 X5 X4
+"""
 
 
 def tile_quietstarthoughtmixinghead_x2_kernel(
@@ -57,34 +70,27 @@ def tile_quietstarthoughtmixinghead_x2_kernel(
         nc.vector.memset(e_sc[:].bitcast(I32), 0)
         nc.vector.memset(ones[:], 1.0)
 
-        def load_rows(src, g, pair, nm):
-            dst = keep.tile([P, 2, D], BF16, align_bytes=64, name=nm)
-            view = src[512 * g : 512 * g + 512, :].rearrange("(p s) c -> p s c", s=4)
-            nc.sync.dma_start(out=dst[:], in_=view[:, 2 * pair : 2 * pair + 2, :])
-            return dst
+        make_identity(nc, ident[:])
+        nc.gpsimd.dma_start(out=vg_row[0:1, 0:F], in_=v.unsqueeze(0))
+        nc.gpsimd.dma_start(out=vg_row[0:1, F : F + D], in_=gain.unsqueeze(0))
 
-        def load_words(src, n, nm, width=N):
-            dst = keep.tile([P, 2, width], U32, align_bytes=64, name=nm)
+        rows = {}
+        words = {}
+        sources = {"h": h, "t": t}
+
+        def load_rows(x, pair, first, count):
+            if (x, pair) not in rows:
+                rows[x, pair] = keep.tile([P, 2, D], BF16, align_bytes=64, name="%s_sb%d" % (x, pair))
+            g = pair // 2
+            view = sources[x][512 * g : 512 * g + 512, :].rearrange("(p s) c -> p s c", s=4)
+            s = 2 * (pair % 2) + first
+            nc.sync.dma_start(out=rows[x, pair][:, first : first + count, :], in_=view[:, s : s + count, :])
+
+        def load_words(src, n, nm, width):
+            dst = keep.tile([P, 2, width], U32, align_bytes=64, name="words_%s%d" % (nm, n))
             view = src.rearrange("g p n b -> p g (n b)")[:, :, 4 * width * n : 4 * width * (n + 1)]
             nc.sync.dma_start(out=dst[:].bitcast(I32), in_=view.bitcast(I32))
-            return dst
-
-        h_sb, t_sb, wa_sb, wb_sb, e_sb = {}, {}, {}, {}, {}
-        make_identity(nc, ident[:])
-        for q in range(4):
-            nc.scalar.dma_start(
-                out=w_sc[32 * q : 32 * q + 8, :].bitcast(I32), in_=wa_scales[:, 4 * q : 4 * q + 4, :].bitcast(I32)
-            )
-        nc.scalar.dma_start(out=vg_row[0:1, 0:F], in_=v.unsqueeze(0))
-        nc.scalar.dma_start(out=vg_row[0:1, F : F + D], in_=gain.unsqueeze(0))
-
-        def load_pair(i):
-            h_sb[i] = load_rows(h, i // 2, i % 2, "h_sb%d" % i)
-            t_sb[i] = load_rows(t, i // 2, i % 2, "t_sb%d" % i)
-
-        def load_weights(n):
-            wa_sb[n] = load_words(wa_words, n, "wa_sb%d" % n)
-            wb_sb[n] = load_words(wb_words, n, "wb_sb%d" % n)
+            words[nm, n] = dst
 
         def load_wb_scales():
             for q in range(4):
@@ -93,114 +99,136 @@ def tile_quietstarthoughtmixinghead_x2_kernel(
                     in_=wb_scales[:, 4 * q : 4 * q + 4, :].bitcast(I32),
                 )
 
+        def load_pair(pair):
+            load_rows("h", pair, 0, 2)
+            load_rows("t", pair, 0, 2)
+
+        def load_weights(n):
+            load_words(wa_words, n, "h", N)
+            load_words(wb_words, n, "t", N)
+
         def load_e():
             for q in range(4):
                 nc.sync.dma_start(
                     out=e_sc[32 * q : 32 * q + 8, :].bitcast(I32), in_=e_scales[:, 4 * q : 4 * q + 4, :].bitcast(I32)
                 )
             for n in range(2):
-                e_sb[n] = load_words(e_words, n, "e_sb%d" % n, 2 * N)
+                load_words(e_words, n, "e", 2 * N)
 
-        if LOADS == "C":
-            for nm, src, group in (("h", h, h_sb), ("t", t, t_sb)):
-                group[0] = keep.tile([P, 2, D], BF16, align_bytes=64, name="%s_sb0" % nm)
-                view = src[0:512, :].rearrange("(p s) c -> p s c", s=4)
-                nc.sync.dma_start(out=group[0][:, 0, :], in_=view[:, 0, :])
-            load_wb_scales()
+        def load_small():
+            for q in range(4):
+                nc.scalar.dma_start(
+                    out=w_sc[32 * q : 32 * q + 8, :].bitcast(I32), in_=wa_scales[:, 4 * q : 4 * q + 4, :].bitcast(I32)
+                )
+
+        if LOADS in ("C", "D"):
+            load_rows("h", 0, 0, 1)
+            load_rows("t", 0, 0, 1)
             load_weights(0)
-            for src, group in ((h, h_sb), (t, t_sb)):
-                view = src[0:512, :].rearrange("(p s) c -> p s c", s=4)
-                nc.sync.dma_start(out=group[0][:, 1, :], in_=view[:, 1, :])
-            load_weights(1)
-            load_pair(1)
+            load_small()
+            load_wb_scales()
+            load_rows("h", 0, 1, 1)
+            load_rows("t", 0, 1, 1)
+            if LOADS == "C":
+                load_weights(1)
+                load_pair(1)
+                load_pair(2)
+                load_e()
+            else:
+                load_pair(1)
+                load_weights(1)
+                load_e()
+                load_pair(2)
         else:
             load_pair(0)
+            load_small()
             load_wb_scales()
-        if LOADS == "C":
-            pass
-        elif LOADS == "B":
-            load_pair(1)
-            load_weights(0)
-            load_weights(1)
-        else:
-            load_weights(0)
-            load_weights(1)
-            load_pair(1)
-        load_pair(2)
-        load_e()
+            if LOADS == "B":
+                load_pair(1)
+                load_weights(0)
+                load_weights(1)
+            else:
+                load_weights(0)
+                load_weights(1)
+                load_pair(1)
+            load_pair(2)
+            load_e()
         load_pair(3)
-        rows = {"h": h_sb, "t": t_sb}
-        weights = {"h": wa_sb, "t": wb_sb}
 
         nc.scalar.activation(out=warm_out[:], in_=warm[:], func=ACT.Sigmoid)
 
         def row_of(x, b):
-            return rows[x][b // 2][:, b % 2, :]
+            return rows[x, b // 2][:, b % 2, :]
 
-        grouped, codes, scales = {}, {}, {}
+        bank_of, grouped, codes, scales = {}, {}, {}, {}
+        hidden, logit, gate_w, gate_u, kept, mixed, gained, early = {}, {}, {}, {}, {}, {}, {}, {}
+        out_f, out_s, out_b, out_c = {}, {}, {}, {}
+        quantised = set()
 
-        def copy_grouped(dst, bank):
-            nc.scalar.copy(
-                out=dst[:].bitcast(F32).rearrange("p (g r u) -> p g r u", g=2, u=2),
-                in_=bank[:].rearrange("p (g u r) -> p g r u", g=2, u=2),
-            )
+        def spread(c):
+            bank_of["sp", c] = psum.tile([P, N], F32, name="bank_t", tag="bank_t", bufs=BANKS[0])
+            nc.tensor.matmul(bank_of["sp", c][:], lhsT=ones[:], rhs=vg_row[:, N * c : N * (c + 1)], start=True, stop=True)
 
-        permuted = {}
-
-        def perm(x, pair):
-            dst = work.tile([P, 2, 512], F32, align_bytes=64, name="pw", tag="pw", bufs=2)
-            nc.vector.tensor_copy(
-                out=dst[:].rearrange("p s (u k) -> p s u k", u=2),
-                in_=rows[x][pair][:].bitcast(F32).rearrange("p s (k u) -> p s u k", u=2),
-            )
-            permuted[x, pair] = dst
+        def spread_copy(c):
+            bank = bank_of["sp", c]
+            if c == 0:
+                nc.scalar.copy(out=v_b[:, 0:N], in_=bank[:])
+            elif c == 1:
+                nc.scalar.activation(out=v_b[:, N:F], in_=bank[:], func=ACT.Copy, scale=-1.0)
+            else:
+                nc.scalar.copy(
+                    out=gain_b[:].rearrange("p (u g k e) -> p u g k e", u=2, g=2, e=2)[:, :, c - 2, :, :],
+                    in_=bank[:].rearrange("p (k u e) -> p u k e", u=2, e=2),
+                )
 
         def turn(x, b):
-            if (x, b // 2) in permuted:
-                words = permuted[x, b // 2][:, b % 2, :]
-            else:
-                words = row_of(x, b).bitcast(F32)
             bank = psum.tile([P, N], F32, name="bank_t", tag="bank_t", bufs=BANKS[0])
+            src = gained[b][:].bitcast(F32) if x == "m" else row_of(x, b).bitcast(F32)
             for g in range(2):
                 for u in range(2):
                     lo = (2 * g + u) * P
-                    if (x, b // 2) in permuted:
-                        part = words[:, 256 * u + P * g : 256 * u + P * (g + 1)]
+                    if x == "m":
+                        part = src[:, 256 * u + P * g : 256 * u + P * (g + 1)]
                     else:
-                        part = words[:, 256 * g + u : 256 * (g + 1) : 2]
+                        part = src[:, 256 * g + u : 256 * (g + 1) : 2]
                     nc.tensor.transpose(bank[:, lo : lo + P], part, ident[:])
-            dst = work.tile([P, D], BF16, align_bytes=64, name="gr", tag="gr", bufs=4)
-            copy_grouped(dst, bank)
+            bank_of[x, b] = bank
+
+        def group(x, b):
+            tag = "gm" if x == "m" else "gr"
+            dst = work.tile([P, D], BF16, align_bytes=64, name=tag, tag=tag, bufs=BUFS[tag])
+            nc.scalar.copy(
+                out=dst[:].bitcast(F32).rearrange("p (g r u) -> p g r u", g=2, u=2),
+                in_=bank_of[x, b][:].rearrange("p (g u r) -> p g r u", g=2, u=2),
+            )
             grouped[x, b] = dst
 
         def quant(x, b):
-            c = work.tile([P, 256], U32, align_bytes=64, name="cd", tag="cd", bufs=8)
-            s = work.tile([P, 256], U8, align_bytes=64, name="sc", tag="sc", bufs=8)
+            tag = "mq" if x == "m" else "hq"
+            c = work.tile([P, 256], U32, align_bytes=64, name=tag, tag=tag, bufs=BUFS[tag])
+            s = work.tile([P, 256], U8, align_bytes=64, name=tag + "s", tag=tag + "s", bufs=BUFS[tag])
             nc.vector.quantize_mx(out=c[:].bitcast(FP8X4), scales=s[:], in_=grouped[x, b][:])
             codes[x, b], scales[x, b] = c, s
 
-        hidden, logit, w_t, a_t, m_t, mg_t = {}, {}, {}, {}, {}, {}
-
-        def stage1(b, hf):
-            acc = psum.tile([P, N], F32, name="bank_1", tag="bank_1", bufs=BANKS[1])
+        def stage1(x, b, hf):
+            if x == "h":
+                hidden[b, hf] = psum.tile([P, N], F32, name="bank_1", tag="bank_1", bufs=BANKS[1])
             cols = slice(N * hf, N * (hf + 1))
-            for i, x in enumerate("ht"):
-                for g in range(2):
-                    k = 4 * (2 * i + g)
-                    nc.tensor.matmul_mx(
-                        out=acc[:],
-                        lhsT=codes[x, b][:, P * g : P * (g + 1)].bitcast(FP8X4),
-                        lhsT_scale=scales[x, b][:, P * g : P * (g + 1)],
-                        rhs=weights[x][hf][:, g, :].bitcast(FP8X4),
-                        rhs_scale=w_sc[k:P, cols],
-                        start=(k == 0),
-                        stop=(k == 12),
-                    )
-            hidden[b, hf] = acc
+            for g in range(2):
+                k = 4 * (2 * "ht".index(x) + g)
+                nc.tensor.matmul_mx(
+                    out=hidden[b, hf][:],
+                    lhsT=codes[x, b][:, P * g : P * (g + 1)].bitcast(FP8X4),
+                    lhsT_scale=scales[x, b][:, P * g : P * (g + 1)],
+                    rhs=words[x, hf][:, g, :].bitcast(FP8X4),
+                    rhs_scale=w_sc[k:P, cols],
+                    start=(k == 0),
+                    stop=(k == 12),
+                )
 
         def logits(b, hf):
-            if hf == 0:
-                logit[b] = work.tile([P, 2], F32, align_bytes=64, name="lg", tag="lg", bufs=3)
+            if b not in logit:
+                logit[b] = work.tile([P, 2], F32, align_bytes=64, name="lg", tag="lg", bufs=4)
             junk = work.tile([P, N], F32, align_bytes=64, name="junk", tag="junk", bufs=2)
             nc.vector.scalar_tensor_tensor(
                 out=junk[:],
@@ -213,224 +241,144 @@ def tile_quietstarthoughtmixinghead_x2_kernel(
             )
 
         def gate(b):
+            u = work.tile([P, 1], F32, align_bytes=64, name="ut", tag="ut", bufs=4)
             w = work.tile([P, 1], F32, align_bytes=64, name="wt", tag="wt", bufs=4)
-            u = work.tile([P, 1], F32, align_bytes=64, name="ut", tag="ut", bufs=3)
-            nc.scalar.activation(out=u[:], in_=logit[b][:, 0:1], func=ACT.Sigmoid, bias=logit[b][:, 1:2], scale=-1.0)
-            nc.scalar.activation(out=w[:], in_=logit[b][:, 1:2], func=ACT.Sigmoid, bias=logit[b][:, 0:1], scale=-1.0)
-            a = work.tile([P, D], F32, align_bytes=64, name="at", tag="at", bufs=3)
-            src = gained["h", b][:] if b in EARLY else row_of("h", b)
-            nc.scalar.activation(out=a[:], in_=src, func=ACT.Copy, scale=u[:, 0:1])
-            w_t[b], a_t[b] = w, a
+            first, second = logit[b][:, 0:1], logit[b][:, 1:2]
+            nc.scalar.activation(out=u[:], in_=first, func=ACT.Sigmoid, bias=second, scale=-1.0)
+            nc.scalar.activation(out=w[:], in_=second, func=ACT.Sigmoid, bias=first, scale=-1.0)
+            gate_u[b], gate_w[b] = u, w
 
-        gained = {}
+        def keep_part(b):
+            a = work.tile([P, D], F32, align_bytes=64, name="at", tag="at", bufs=BUFS["at"])
+            src = early["h", b][:] if b in EARLY else row_of("h", b)
+            nc.scalar.activation(out=a[:], in_=src, func=ACT.Copy, scale=gate_u[b][:, 0:1])
+            kept[b] = a
 
         def early_gain(x, b):
-            if b not in EARLY:
-                return
-            dst = work.tile([P, D], F32, align_bytes=64, name="eg", tag="eg", bufs=4)
+            dst = work.tile([P, D], F32, align_bytes=64, name="eg", tag="eg", bufs=BUFS["eg"])
             nc.vector.tensor_tensor(
                 out=dst[:].rearrange("p (u k e) -> p u k e", u=2, e=2),
                 in0=row_of(x, b).rearrange("p (k u e) -> p u k e", u=2, e=2),
                 in1=gain_b[:].rearrange("p (u k e) -> p u k e", u=2, e=2),
                 op=ALU.mult,
             )
-            gained[x, b] = dst
+            early[x, b] = dst
 
         def mix(b):
-            if b in EARLY:
-                return
-            m = work.tile([P, D], F32, align_bytes=64, name="mt", tag="mt", bufs=3)
+            m = work.tile([P, D], F32, align_bytes=64, name="mt", tag="mt", bufs=BUFS["mt"])
             nc.vector.scalar_tensor_tensor(
-                out=m[:], in0=row_of("t", b), scalar=w_t[b][:, 0:1], in1=a_t[b][:], op0=ALU.mult, op1=ALU.add
+                out=m[:], in0=row_of("t", b), scalar=gate_w[b][:, 0:1], in1=kept[b][:], op0=ALU.mult, op1=ALU.add
             )
-            m_t[b] = m
+            mixed[b] = m
 
         def gains(b):
-            mg = work.tile([P, D], BF16, align_bytes=64, name="mg", tag="mg", bufs=3)
-            mg_t[b] = mg
+            mg = work.tile([P, D], BF16, align_bytes=64, name="mg", tag="mg", bufs=BUFS["mg"])
+            gained[b] = mg
             if b in EARLY:
                 nc.vector.scalar_tensor_tensor(
-                    out=mg[:], in0=gained["t", b][:], scalar=w_t[b][:, 0:1], in1=a_t[b][:], op0=ALU.mult, op1=ALU.add
+                    out=mg[:], in0=early["t", b][:], scalar=gate_w[b][:, 0:1], in1=kept[b][:], op0=ALU.mult, op1=ALU.add
                 )
-                return
-            nc.vector.tensor_tensor(
-                out=mg[:].rearrange("p (u k e) -> p u k e", u=2, e=2),
-                in0=m_t[b][:].rearrange("p (k u e) -> p u k e", u=2, e=2),
-                in1=gain_b[:].rearrange("p (u k e) -> p u k e", u=2, e=2),
-                op=ALU.mult,
-            )
-
-        def turn_mixed(b):
-            words = mg_t[b][:].bitcast(F32)
-            bank = psum.tile([P, N], F32, name="bank_t", tag="bank_t", bufs=BANKS[0])
-            for g in range(2):
-                for u in range(2):
-                    lo = (2 * g + u) * P
-                    nc.tensor.transpose(bank[:, lo : lo + P], words[:, 256 * u + P * g : 256 * u + P * (g + 1)], ident[:])
-            dst = work.tile([P, D], BF16, align_bytes=64, name="gm", tag="gm", bufs=3)
-            copy_grouped(dst, bank)
-            grouped["m", b] = dst
-
-        out_f, out_s = {}, {}
-        stored = set()
+            else:
+                nc.vector.tensor_tensor(
+                    out=mg[:].rearrange("p (u k e) -> p u k e", u=2, e=2),
+                    in0=mixed[b][:].rearrange("p (k u e) -> p u k e", u=2, e=2),
+                    in1=gain_b[:].rearrange("p (u k e) -> p u k e", u=2, e=2),
+                    op=ALU.mult,
+                )
 
         def stage2(b, n):
-            g, s = divmod(b, 4)
-            if g not in out_f:
-                out_f[g] = keep.tile([P, 4, V], F32, align_bytes=64, name="out_f%d" % g)
-                out_s[g] = keep.tile([P, V], U8, align_bytes=64, name="out_s%d" % g)
             acc = psum.tile([P, N], F32, name="bank_2", tag="bank_2", bufs=BANKS[2])
-            cols = slice(N * n, N * (n + 1))
             for k in range(2):
                 nc.tensor.matmul_mx(
                     out=acc[:],
                     lhsT=codes["m", b][:, P * k : P * (k + 1)].bitcast(FP8X4),
                     lhsT_scale=scales["m", b][:, P * k : P * (k + 1)],
-                    rhs=e_sb[n // 2][:, k, N * (n % 2) : N * (n % 2 + 1)].bitcast(FP8X4),
-                    rhs_scale=e_sc[4 * k : P, cols],
+                    rhs=words["e", n // 2][:, k, N * (n % 2) : N * (n % 2 + 1)].bitcast(FP8X4),
+                    rhs_scale=e_sc[4 * k : P, N * n : N * (n + 1)],
                     start=(k == 0),
                     stop=(k == 1),
                 )
-            nc.scalar.copy(out=out_f[g][:, s, cols], in_=acc[:])
-            stored.add((b, n))
+            bank_of["o", b, n] = acc
+
+        def store_out(b, n):
+            g, s = divmod(b, 4)
+            if (g, n) not in out_f:
+                out_f[g, n] = keep.tile([P, 4, N], F32, align_bytes=64, name="out_f%d%d" % (g, n))
+            if g not in out_s:
+                out_s[g] = keep.tile([P, V], U8, align_bytes=64, name="out_s%d" % g)
+            nc.scalar.copy(out=out_f[g, n][:, s, :], in_=bank_of["o", b, n][:])
             view = out_0[512 * g : 512 * g + 512, :].rearrange("(p s) m -> p s m", s=4)
-            if S2ORD[g] == "chunk":
-                if s == 3:
-                    nc.sync.dma_start(out=view[:, :, cols], in_=out_f[g][:, :, cols])
-            elif b < WIDE and n == 3:
-                nc.sync.dma_start(out=view[:, s, :], in_=out_f[g][:, s, :])
-            elif b >= WIDE and n % 2 == 1:
-                pair = slice(N * (n - 1), N * (n + 1))
-                nc.sync.dma_start(out=view[:, s, pair], in_=out_f[g][:, s, pair])
+            nc.sync.dma_start(out=view[:, s, N * n : N * (n + 1)], in_=out_f[g, n][:, s, :])
 
-        out_b, out_c = {}, {}
-
-        def interleave(g, n, engine):
-            ob = work.tile([P, N, 4], BF16, align_bytes=64, name="ob", tag="ob", bufs=3)
+        def interleave(i):
+            g, n = divmod(i, 4)
+            engine = nc.scalar.copy if i in F_ON_S else nc.vector.tensor_copy
+            ob = work.tile([P, N, 4], BF16, align_bytes=64, name="ob", tag="ob", bufs=BUFS["ob"])
             engine(
                 out=ob[:].rearrange("p (c i) s -> p c s i", i=4),
-                in_=out_f[g][:, :, N * n : N * (n + 1)].rearrange("p s (c i) -> p c s i", i=4),
+                in_=out_f[g, n][:].rearrange("p s (c i) -> p c s i", i=4),
             )
-            out_b[g, n] = ob
+            out_b[i] = ob
 
-        def quant_out(g, n):
-            if n % 2 == 0:
-                out_c[g] = work.tile([P, 2 * N], U32, align_bytes=64, name="oc", tag="oc", bufs=2)
+        def quant_out(i):
+            g, n = divmod(i, 4)
+            if (g, n // 2) not in out_c:
+                out_c[g, n // 2] = work.tile([P, 2 * N], U32, align_bytes=64, name="oc", tag="oc", bufs=2)
+            oc = out_c[g, n // 2]
             half = slice(N * (n % 2), N * (n % 2 + 1))
-            oc = out_c[g]
             nc.vector.quantize_mx(
                 out=oc[:, half].bitcast(FP8X4),
                 scales=out_s[g][:, N * n : N * (n + 1)],
-                in_=out_b[g, n][:].rearrange("p m s -> p (m s)"),
+                in_=out_b[i][:].rearrange("p m s -> p (m s)"),
             )
-            words_view = out_1[g].rearrange("p m b -> p (m b)")
-            if (g, n) in ((1, 2), (1, 3)):
-                part = words_view[:, 4 * N * n : 4 * N * (n + 1)]
-                nc.sync.dma_start(out=part.bitcast(I32), in_=oc[:, half].bitcast(I32))
-            elif n % 2 == 1:
-                part = words_view[:, 4 * N * (n - 1) : 4 * N * (n + 1)]
-                nc.sync.dma_start(out=part.bitcast(I32), in_=oc[:].bitcast(I32))
-            if n == 3:
+            quantised.add(i)
+            view = out_1[g].rearrange("p m b -> p (m b)")
+            nc.sync.dma_start(
+                out=view[:, 4 * N * n : 4 * N * (n + 1)].bitcast(I32), in_=oc[:, half].bitcast(I32)
+            )
+            if all(4 * g + k in quantised for k in range(4)):
                 for q in range(4):
                     nc.sync.dma_start(
                         out=out_2[g, 4 * q : 4 * q + 4, :].bitcast(I32),
                         in_=out_s[g][32 * q : 32 * q + 4, :].bitcast(I32),
                     )
 
-        def spread():
-            for c in range(4):
-                bank = psum.tile([P, N], F32, name="bank_t", tag="bank_t", bufs=BANKS[0])
-                nc.tensor.matmul(bank[:], lhsT=ones[:], rhs=vg_row[:, N * c : N * (c + 1)], start=True, stop=True)
-                if c == 0:
-                    nc.scalar.copy(out=v_b[:, 0:N], in_=bank[:])
-                elif c == 1:
-                    nc.scalar.activation(out=v_b[:, N:F], in_=bank[:], func=ACT.Copy, scale=-1.0)
-                else:
-                    nc.scalar.copy(
-                        out=gain_b[:].rearrange("p (u g k e) -> p u g k e", u=2, g=2, e=2)[:, :, c - 2, :, :],
-                        in_=bank[:].rearrange("p (k u e) -> p u k e", u=2, e=2),
-                    )
-
-        done = []
-        stream = []
-        for g in range(2):
-            if S2ORD[g] == "b":
-                stream += [(4 * g + s, n) for s in range(4) for n in range(4)]
-            elif S2ORD[g] == "late":
-                stream += [(4 * g + s, n) for s in range(2) for n in range(4)]
-                stream += [(4 * g + s, n) for n in range(4) for s in (2, 3)]
-            elif S2ORD[g] == "late3":
-                stream += [(4 * g + s, n) for s in range(1) for n in range(4)]
-                stream += [(4 * g + s, n) for n in range(4) for s in (1, 2, 3)]
-            elif S2ORD[g] == "pair":
-                stream += [(4 * g + s, 2 * c + n) for c in range(2) for s in range(4) for n in range(2)]
-            else:
-                stream += [(4 * g + s, n) for n in range(4) for s in range(4)]
-        late_i = []
-        late_q = []
-
-        def fill_i():
-            i = len(late_i)
-            if i < 8 and all((4 * (i // 4) + s, i % 4) in stored for s in range(4)):
-                g, n = divmod(i, 4)
-                interleave(g, n, nc.scalar.copy if i in F_ON_S else nc.vector.tensor_copy)
-                late_i.append(i)
-
-        def fill_q():
-            i = len(late_q)
-            if i < len(late_i):
-                quant_out(*divmod(i, 4))
-                late_q.append(i)
-
-        for k in STEPS:
-            for piece, off, arg in PLAN:
-                b = k + off
-                if piece == "fi":
-                    if k >= off:
-                        fill_i()
-                    continue
-                if piece == "fq":
-                    if k >= off:
-                        fill_q()
-                    continue
-                if piece == "s2":
-                    for i in range(arg):
-                        if k >= off and stream and ("m", stream[0][0]) in codes:
-                            stage2(*stream.pop(0))
-                    continue
-                if piece == "perm":
-                    if b % 2 == 0 and b // 2 in PERM and 0 <= b < BLOCKS:
-                        perm(arg, b // 2)
-                    continue
-                if not 0 <= b < BLOCKS:
-                    continue
-                if piece == "turn":
-                    turn(arg, b)
-                elif piece == "quant":
-                    quant(arg, b)
-                elif piece == "pre":
-                    if not done:
-                        spread()
-                        done.append(1)
-                    early_gain(arg, b)
-                elif piece == "stage1":
-                    if not done:
-                        spread()
-                        done.append(1)
-                    stage1(b, arg)
-                elif piece == "logits":
-                    logits(b, arg)
-                elif piece == "gate":
-                    gate(b)
-                elif piece == "mix":
-                    mix(b)
-                elif piece == "gains":
-                    gains(b)
-                elif piece == "turn_mixed":
-                    turn_mixed(b)
-        while len(late_q) < 8:
-            if stream:
-                stage2(*stream.pop(0))
-                continue
-            fill_i()
-            fill_q()
+        for item in ORDER.split():
+            d = [int(c) for c in item if c in "01234567"]
+            name = item[: len(item) - len(d)]
+            if name == "sp":
+                spread(d[0])
+            elif name == "spc":
+                spread_copy(d[0])
+            elif name in ("Th", "Tt"):
+                turn(name[1], d[0])
+            elif name == "M":
+                turn("m", d[0])
+            elif name in ("Gh", "Gt", "Gm"):
+                group(name[1], d[0])
+            elif name in ("Qh", "Qt", "Qm"):
+                quant(name[1], d[0])
+            elif name == "U":
+                stage1("h", d[0], d[1])
+            elif name == "W":
+                stage1("t", d[0], d[1])
+            elif name == "L":
+                logits(d[0], d[1])
+            elif name == "g":
+                gate(d[0])
+            elif name == "A":
+                keep_part(d[0])
+            elif name in ("eh", "et"):
+                early_gain(name[1], d[0])
+            elif name == "m":
+                mix(d[0])
+            elif name == "n":
+                gains(d[0])
+            elif name == "S":
+                stage2(d[0], d[1])
+            elif name == "O":
+                store_out(d[0], d[1])
+            elif name == "F":
+                interleave(d[0])
+            elif name == "X":
+                quant_out(d[0])

from contextlib import ExitStack

import concourse.mybir as mybir
from concourse.masks import make_identity

FLOPS = 2 * 1024 * 2048 * 1024 + 2 * 1024 * 1024 * 2048

F32 = mybir.dt.float32
BF16 = mybir.dt.bfloat16
U32 = mybir.dt.uint32
I32 = mybir.dt.int32
U8 = mybir.dt.uint8
FP8X4 = mybir.dt.float8_e4m3fn_x4
ALU = mybir.AluOpType
ACT = mybir.ActivationFunctionType

P = 128
D = 1024
F = 1024
V = 2048
N = 512
BLOCKS = 8
BANKS = (3, 2, 3)
LOADS = "C"
F_ON_S = (6,)
EARLY = ()
BUFS = dict(gr=5, hq=10, at=3, mt=2, mg=3, gm=3, mq=6, ob=4, eg=4)
ORDER = """
    Th0 Tt0 Gh0 Gt0 sp1 sp0 Qt0 Qh0 U00 W00 sp2 spc1 spc0 spc2 Th1 Tt1
    U01 sp3 W01 Gh1 Gt1 spc3 L00 Qh1 L01 Qt1 U11 Th3 U10 W10 Th2 Tt2
    g0 A0 Gh3 Gh2 Gt2 Tt3 W11 m0 Qh3 Qh2 L10 L11 Gt3 Th5 Th4 Tt4
    U21 Gt4 Gh5 Gh4 g1 A1 Qt2 n0 Qt4 Qt3 U20 W21 W20 Tt5 M0 L21
    L20 m1 U31 W31 U30 g2 Gm0 Gt5 Th7 Th6 Tt6 Gh7 Gh6 A2 Qm0 L31
    Qh5 Qh4 n1 W30 S02 S00 U41 S03 Qt5 Qh7 L30 m2 n2 W41 U40 W40
    O00 g3 O02 Gt6 O03 A3 Tt7 M1 M2 L41 Qt6 L40 m3 U51 W51 U50
    W50 S01 Gm1 g4 Gm2 Gt7 A4 Qm1 Qh6 L51 L50 n3 m4 Qm2 S12 S13
    U61 U60 W61 W60 L61 L60 Qt7 n4 O12 O01 O13 g5 A5 M3 S23 S22
    S11 U70 g6 O23 O22 A6 Gm3 O11 m5 n5 S10 S21 W70 U71 W71 S20
    O21 O10 O20 M4 M5 L70 Qm3 L71 Gm4 Gm5 g7 m6 Qm4 n6 Qm5 S33
    S43 S32 O33 A7 O43 O32 S53 M6 F3 m7 S31 O53 Gm6 S42 S52 O31
    O42 S41 F2 Qm6 O52 S30 O41 S63 O30 S62 O63 n7 X2 O62 S40 M7
    S51 S61 O40 Gm7 O51 S60 S50 O61 O60 O50 X3 F1 Qm7 F0 X1 X0
    S73 S70 S71 O73 O70 S72 F7 O71 O72 F4 F5 F6 X7 X6 X5 X4
"""


def tile_quietstarthoughtmixinghead_x2_kernel(
    tc, h, t, wa_words, wa_scales, wb_words, wb_scales, v, gain, e_words, e_scales, out_0, out_1, out_2
):
    nc = tc.nc
    with ExitStack() as ctx:
        keep = ctx.enter_context(tc.tile_pool(name="keep", bufs=1))
        work = ctx.enter_context(tc.tile_pool(name="work", bufs=3))
        psum = ctx.enter_context(tc.psum_pool(name="psum", bufs=1))
        ctx.enter_context(tc.manual_schedule())

        w_sc = keep.tile([P, F], U8, align_bytes=64, name="w_sc")
        e_sc = keep.tile([P, V], U8, align_bytes=64, name="e_sc")
        vg_row = keep.tile([P, 2 * D], BF16, align_bytes=64, name="vg_row")
        ones = keep.tile([P, P], BF16, align_bytes=64, name="ones")
        warm = keep.tile([P, 1], F32, align_bytes=64, name="warm")
        warm_out = keep.tile([P, 1], F32, align_bytes=64, name="warm_out")
        ident = keep.tile([P, P], F32, align_bytes=64, name="ident")
        v_b = keep.tile([P, F], BF16, align_bytes=64, name="v_b")
        gain_b = keep.tile([P, D], BF16, align_bytes=64, name="gain_b")

        nc.vector.memset(w_sc[:].bitcast(I32), 0)
        nc.vector.memset(vg_row[:], 0.0)
        nc.vector.memset(warm[:], 0.0)
        nc.vector.memset(e_sc[:].bitcast(I32), 0)
        nc.vector.memset(ones[:], 1.0)

        make_identity(nc, ident[:])
        nc.gpsimd.dma_start(out=vg_row[0:1, 0:F], in_=v.unsqueeze(0))
        nc.gpsimd.dma_start(out=vg_row[0:1, F : F + D], in_=gain.unsqueeze(0))

        rows = {}
        words = {}
        sources = {"h": h, "t": t}

        def load_rows(x, pair, first, count):
            if (x, pair) not in rows:
                rows[x, pair] = keep.tile([P, 2, D], BF16, align_bytes=64, name="%s_sb%d" % (x, pair))
            g = pair // 2
            view = sources[x][512 * g : 512 * g + 512, :].rearrange("(p s) c -> p s c", s=4)
            s = 2 * (pair % 2) + first
            nc.sync.dma_start(out=rows[x, pair][:, first : first + count, :], in_=view[:, s : s + count, :])

        def load_words(src, n, nm, width):
            dst = keep.tile([P, 2, width], U32, align_bytes=64, name="words_%s%d" % (nm, n))
            view = src.rearrange("g p n b -> p g (n b)")[:, :, 4 * width * n : 4 * width * (n + 1)]
            nc.sync.dma_start(out=dst[:].bitcast(I32), in_=view.bitcast(I32))
            words[nm, n] = dst

        def load_wb_scales():
            for q in range(4):
                nc.sync.dma_start(
                    out=w_sc[32 * q + 8 : 32 * q + 16, :].bitcast(I32),
                    in_=wb_scales[:, 4 * q : 4 * q + 4, :].bitcast(I32),
                )

        def load_pair(pair):
            load_rows("h", pair, 0, 2)
            load_rows("t", pair, 0, 2)

        def load_weights(n):
            load_words(wa_words, n, "h", N)
            load_words(wb_words, n, "t", N)

        def load_e():
            for q in range(4):
                nc.sync.dma_start(
                    out=e_sc[32 * q : 32 * q + 8, :].bitcast(I32), in_=e_scales[:, 4 * q : 4 * q + 4, :].bitcast(I32)
                )
            for n in range(2):
                load_words(e_words, n, "e", 2 * N)

        def load_small():
            for q in range(4):
                nc.scalar.dma_start(
                    out=w_sc[32 * q : 32 * q + 8, :].bitcast(I32), in_=wa_scales[:, 4 * q : 4 * q + 4, :].bitcast(I32)
                )

        if LOADS in ("C", "D"):
            load_rows("h", 0, 0, 1)
            load_rows("t", 0, 0, 1)
            load_weights(0)
            load_small()
            load_wb_scales()
            load_rows("h", 0, 1, 1)
            load_rows("t", 0, 1, 1)
            if LOADS == "C":
                load_weights(1)
                load_pair(1)
                load_pair(2)
                load_e()
            else:
                load_pair(1)
                load_weights(1)
                load_e()
                load_pair(2)
        else:
            load_pair(0)
            load_small()
            load_wb_scales()
            if LOADS == "B":
                load_pair(1)
                load_weights(0)
                load_weights(1)
            else:
                load_weights(0)
                load_weights(1)
                load_pair(1)
            load_pair(2)
            load_e()
        load_pair(3)

        nc.scalar.activation(out=warm_out[:], in_=warm[:], func=ACT.Sigmoid)

        def row_of(x, b):
            return rows[x, b // 2][:, b % 2, :]

        bank_of, grouped, codes, scales = {}, {}, {}, {}
        hidden, logit, gate_w, gate_u, kept, mixed, gained, early = {}, {}, {}, {}, {}, {}, {}, {}
        out_f, out_s, out_b, out_c = {}, {}, {}, {}
        quantised = set()

        def spread(c):
            bank_of["sp", c] = psum.tile([P, N], F32, name="bank_t", tag="bank_t", bufs=BANKS[0])
            nc.tensor.matmul(bank_of["sp", c][:], lhsT=ones[:], rhs=vg_row[:, N * c : N * (c + 1)], start=True, stop=True)

        def spread_copy(c):
            bank = bank_of["sp", c]
            if c == 0:
                nc.scalar.copy(out=v_b[:, 0:N], in_=bank[:])
            elif c == 1:
                nc.scalar.activation(out=v_b[:, N:F], in_=bank[:], func=ACT.Copy, scale=-1.0)
            else:
                nc.scalar.copy(
                    out=gain_b[:].rearrange("p (u g k e) -> p u g k e", u=2, g=2, e=2)[:, :, c - 2, :, :],
                    in_=bank[:].rearrange("p (k u e) -> p u k e", u=2, e=2),
                )

        def turn(x, b):
            bank = psum.tile([P, N], F32, name="bank_t", tag="bank_t", bufs=BANKS[0])
            src = gained[b][:].bitcast(F32) if x == "m" else row_of(x, b).bitcast(F32)
            for g in range(2):
                for u in range(2):
                    lo = (2 * g + u) * P
                    if x == "m":
                        part = src[:, 256 * u + P * g : 256 * u + P * (g + 1)]
                    else:
                        part = src[:, 256 * g + u : 256 * (g + 1) : 2]
                    nc.tensor.transpose(bank[:, lo : lo + P], part, ident[:])
            bank_of[x, b] = bank

        def group(x, b):
            tag = "gm" if x == "m" else "gr"
            dst = work.tile([P, D], BF16, align_bytes=64, name=tag, tag=tag, bufs=BUFS[tag])
            nc.scalar.copy(
                out=dst[:].bitcast(F32).rearrange("p (g r u) -> p g r u", g=2, u=2),
                in_=bank_of[x, b][:].rearrange("p (g u r) -> p g r u", g=2, u=2),
            )
            grouped[x, b] = dst

        def quant(x, b):
            tag = "mq" if x == "m" else "hq"
            c = work.tile([P, 256], U32, align_bytes=64, name=tag, tag=tag, bufs=BUFS[tag])
            s = work.tile([P, 256], U8, align_bytes=64, name=tag + "s", tag=tag + "s", bufs=BUFS[tag])
            nc.vector.quantize_mx(out=c[:].bitcast(FP8X4), scales=s[:], in_=grouped[x, b][:])
            codes[x, b], scales[x, b] = c, s

        def stage1(x, b, hf):
            if x == "h":
                hidden[b, hf] = psum.tile([P, N], F32, name="bank_1", tag="bank_1", bufs=BANKS[1])
            cols = slice(N * hf, N * (hf + 1))
            for g in range(2):
                k = 4 * (2 * "ht".index(x) + g)
                nc.tensor.matmul_mx(
                    out=hidden[b, hf][:],
                    lhsT=codes[x, b][:, P * g : P * (g + 1)].bitcast(FP8X4),
                    lhsT_scale=scales[x, b][:, P * g : P * (g + 1)],
                    rhs=words[x, hf][:, g, :].bitcast(FP8X4),
                    rhs_scale=w_sc[k:P, cols],
                    start=(k == 0),
                    stop=(k == 12),
                )

        def logits(b, hf):
            if b not in logit:
                logit[b] = work.tile([P, 2], F32, align_bytes=64, name="lg", tag="lg", bufs=4)
            junk = work.tile([P, N], F32, align_bytes=64, name="junk", tag="junk", bufs=2)
            nc.vector.scalar_tensor_tensor(
                out=junk[:],
                in0=hidden[b, hf][:],
                scalar=0.0,
                in1=v_b[:, N * hf : N * (hf + 1)],
                op0=ALU.max,
                op1=ALU.mult,
                accum_out=logit[b][:, hf : hf + 1],
            )

        def gate(b):
            u = work.tile([P, 1], F32, align_bytes=64, name="ut", tag="ut", bufs=4)
            w = work.tile([P, 1], F32, align_bytes=64, name="wt", tag="wt", bufs=4)
            first, second = logit[b][:, 0:1], logit[b][:, 1:2]
            nc.scalar.activation(out=u[:], in_=first, func=ACT.Sigmoid, bias=second, scale=-1.0)
            nc.scalar.activation(out=w[:], in_=second, func=ACT.Sigmoid, bias=first, scale=-1.0)
            gate_u[b], gate_w[b] = u, w

        def keep_part(b):
            a = work.tile([P, D], F32, align_bytes=64, name="at", tag="at", bufs=BUFS["at"])
            src = early["h", b][:] if b in EARLY else row_of("h", b)
            nc.scalar.activation(out=a[:], in_=src, func=ACT.Copy, scale=gate_u[b][:, 0:1])
            kept[b] = a

        def early_gain(x, b):
            dst = work.tile([P, D], F32, align_bytes=64, name="eg", tag="eg", bufs=BUFS["eg"])
            nc.vector.tensor_tensor(
                out=dst[:].rearrange("p (u k e) -> p u k e", u=2, e=2),
                in0=row_of(x, b).rearrange("p (k u e) -> p u k e", u=2, e=2),
                in1=gain_b[:].rearrange("p (u k e) -> p u k e", u=2, e=2),
                op=ALU.mult,
            )
            early[x, b] = dst

        def mix(b):
            m = work.tile([P, D], F32, align_bytes=64, name="mt", tag="mt", bufs=BUFS["mt"])
            nc.vector.scalar_tensor_tensor(
                out=m[:], in0=row_of("t", b), scalar=gate_w[b][:, 0:1], in1=kept[b][:], op0=ALU.mult, op1=ALU.add
            )
            mixed[b] = m

        def gains(b):
            mg = work.tile([P, D], BF16, align_bytes=64, name="mg", tag="mg", bufs=BUFS["mg"])
            gained[b] = mg
            if b in EARLY:
                nc.vector.scalar_tensor_tensor(
                    out=mg[:], in0=early["t", b][:], scalar=gate_w[b][:, 0:1], in1=kept[b][:], op0=ALU.mult, op1=ALU.add
                )
            else:
                nc.vector.tensor_tensor(
                    out=mg[:].rearrange("p (u k e) -> p u k e", u=2, e=2),
                    in0=mixed[b][:].rearrange("p (k u e) -> p u k e", u=2, e=2),
                    in1=gain_b[:].rearrange("p (u k e) -> p u k e", u=2, e=2),
                    op=ALU.mult,
                )

        def stage2(b, n):
            acc = psum.tile([P, N], F32, name="bank_2", tag="bank_2", bufs=BANKS[2])
            for k in range(2):
                nc.tensor.matmul_mx(
                    out=acc[:],
                    lhsT=codes["m", b][:, P * k : P * (k + 1)].bitcast(FP8X4),
                    lhsT_scale=scales["m", b][:, P * k : P * (k + 1)],
                    rhs=words["e", n // 2][:, k, N * (n % 2) : N * (n % 2 + 1)].bitcast(FP8X4),
                    rhs_scale=e_sc[4 * k : P, N * n : N * (n + 1)],
                    start=(k == 0),
                    stop=(k == 1),
                )
            bank_of["o", b, n] = acc

        def store_out(b, n):
            g, s = divmod(b, 4)
            if (g, n) not in out_f:
                out_f[g, n] = keep.tile([P, 4, N], F32, align_bytes=64, name="out_f%d%d" % (g, n))
            if g not in out_s:
                out_s[g] = keep.tile([P, V], U8, align_bytes=64, name="out_s%d" % g)
            nc.scalar.copy(out=out_f[g, n][:, s, :], in_=bank_of["o", b, n][:])
            view = out_0[512 * g : 512 * g + 512, :].rearrange("(p s) m -> p s m", s=4)
            nc.sync.dma_start(out=view[:, s, N * n : N * (n + 1)], in_=out_f[g, n][:, s, :])

        def interleave(i):
            g, n = divmod(i, 4)
            engine = nc.scalar.copy if i in F_ON_S else nc.vector.tensor_copy
            ob = work.tile([P, N, 4], BF16, align_bytes=64, name="ob", tag="ob", bufs=BUFS["ob"])
            engine(
                out=ob[:].rearrange("p (c i) s -> p c s i", i=4),
                in_=out_f[g, n][:].rearrange("p s (c i) -> p c s i", i=4),
            )
            out_b[i] = ob

        def quant_out(i):
            g, n = divmod(i, 4)
            if (g, n // 2) not in out_c:
                out_c[g, n // 2] = work.tile([P, 2 * N], U32, align_bytes=64, name="oc", tag="oc", bufs=2)
            oc = out_c[g, n // 2]
            half = slice(N * (n % 2), N * (n % 2 + 1))
            nc.vector.quantize_mx(
                out=oc[:, half].bitcast(FP8X4),
                scales=out_s[g][:, N * n : N * (n + 1)],
                in_=out_b[i][:].rearrange("p m s -> p (m s)"),
            )
            quantised.add(i)
            view = out_1[g].rearrange("p m b -> p (m b)")
            nc.sync.dma_start(
                out=view[:, 4 * N * n : 4 * N * (n + 1)].bitcast(I32), in_=oc[:, half].bitcast(I32)
            )
            if all(4 * g + k in quantised for k in range(4)):
                for q in range(4):
                    nc.sync.dma_start(
                        out=out_2[g, 4 * q : 4 * q + 4, :].bitcast(I32),
                        in_=out_s[g][32 * q : 32 * q + 4, :].bitcast(I32),
                    )

        for item in ORDER.split():
            d = [int(c) for c in item if c in "01234567"]
            name = item[: len(item) - len(d)]
            if name == "sp":
                spread(d[0])
            elif name == "spc":
                spread_copy(d[0])
            elif name in ("Th", "Tt"):
                turn(name[1], d[0])
            elif name == "M":
                turn("m", d[0])
            elif name in ("Gh", "Gt", "Gm"):
                group(name[1], d[0])
            elif name in ("Qh", "Qt", "Qm"):
                quant(name[1], d[0])
            elif name == "U":
                stage1("h", d[0], d[1])
            elif name == "W":
                stage1("t", d[0], d[1])
            elif name == "L":
                logits(d[0], d[1])
            elif name == "g":
                gate(d[0])
            elif name == "A":
                keep_part(d[0])
            elif name in ("eh", "et"):
                early_gain(name[1], d[0])
            elif name == "m":
                mix(d[0])
            elif name == "n":
                gains(d[0])
            elif name == "S":
                stage2(d[0], d[1])
            elif name == "O":
                store_out(d[0], d[1])
            elif name == "F":
                interleave(d[0])
            elif name == "X":
                quant_out(d[0])
